import numpy as np
import ml_dtypes


def mxq(x, axis, fmt="e4m3"):
    dtype, down = {"e4m3": (ml_dtypes.float8_e4m3fn, 7), "e5m2": (ml_dtypes.float8_e5m2, 14)}[fmt]
    v = np.moveaxis(np.asarray(x, np.float32).astype(ml_dtypes.bfloat16).astype(np.float64), axis, -1)
    blocks = v.reshape(v.shape[:-1] + (-1, 32))
    amax = np.abs(blocks).max(-1, keepdims=True)
    byte = np.maximum(np.where(amax > 0, np.frexp(amax)[1] - 1 + 127, 0) - down, 1)
    scale = np.exp2(byte - 127.0)
    codes = (blocks / scale).astype(np.float32).astype(dtype).astype(np.float64)
    return np.moveaxis((codes * scale).reshape(v.shape), -1, axis)


WIDE = False


def mx_kscale(k):
    if not WIDE:
        return np.ones(k)
    levels = np.array([10, -10, 5, -5, 0])
    if k % 512:
        return np.exp2(np.random.permutation(np.resize(levels, k // 32))).repeat(32)
    a = np.empty((k // 512, 16))
    for p in range(k // 512):
        a[p, :8] = np.random.permutation(np.resize(levels, 8))
        for g in range(8):
            far = levels[np.abs(levels - a[p, g]) >= 10]
            a[p, g + 8] = far[np.random.randint(len(far))]
    return np.exp2(a.ravel()).repeat(32)


def f64(x):
    return np.asarray(x).astype(np.float64)


def striped8(idx):
    return np.asarray(idx).reshape(8, -1, 16).transpose(0, 2, 1).reshape(128, -1).astype(np.uint16)


def unstriped8(offs):
    return offs.reshape(8, 16, -1).transpose(0, 2, 1).reshape(8, -1).astype(np.int64)


def pick8(x, idx, run):
    r = np.arange(len(x))
    return x[r[:, None], idx[r % (8 * run) // run]]


E2M1 = np.array([0.0, 0.5, 1.0, 1.5, 2.0, 3.0, 4.0, 6.0, -0.0, -0.5, -1.0, -1.5, -2.0, -3.0, -4.0, -6.0])


def pack_weight(w, fmt):
    k, n = w.shape
    w = f64(np.asarray(w, np.float32).astype(ml_dtypes.bfloat16)).reshape(k // 32, 32, n)
    amax = np.abs(w).max(1)
    if fmt == "e4m3":
        byte = np.frexp(amax)[1] - 1 + 127 - 7
    else:
        mant, ex = np.frexp(amax / 6.0)
        byte = np.where(mant > 0.5, ex, ex - 1) + 127
    byte = np.clip(np.where(amax > 0, byte, 1), 1, 254)
    scaled = (w * np.exp2(127.0 - byte)[:, None, :]).reshape(k, n).astype(np.float32)
    by_word = np.ascontiguousarray(scaled.reshape(k // 512, 128, 4, n).transpose(0, 1, 3, 2))
    if fmt == "e4m3":
        words = by_word.astype(ml_dtypes.float8_e4m3fn).view(np.uint8)
    else:
        c = by_word.astype(ml_dtypes.float4_e2m1fn).view(np.uint8) & 0xF
        words = (c[..., 0::2] | (c[..., 1::2] << 4)).reshape(k // 512, 128, 2 * n)
    return np.ascontiguousarray(words), np.ascontiguousarray(byte.astype(np.uint8).reshape(k // 512, 16, n))


def unpack_weight(words, scales, fmt):
    g, _, n = scales.shape
    words = np.ascontiguousarray(words).reshape(g, 128, n, -1)
    if fmt == "e4m3":
        vals = words.view(ml_dtypes.float8_e4m3fn).astype(np.float64)
    else:
        nib = np.empty((g, 128, n, 4), np.uint8)
        nib[..., 0::2] = words & 0xF
        nib[..., 1::2] = words >> 4
        vals = E2M1[nib]
    vals = vals * np.repeat(np.exp2(scales.astype(np.float64) - 127.0), 8, axis=1)[..., None]
    return vals.transpose(0, 1, 3, 2).reshape(g * 512, n)


D, T, U, I, Q = 512, 1024, 1024, 512, 128


def setup_inputs():
    n = np.random.standard_normal
    idx = np.stack([np.random.permutation(T)[:I] for _ in range(8)])
    idx2 = np.stack([np.random.permutation(U)[:I] for _ in range(8)])
    idx3 = np.stack([np.random.permutation(T)[:I] for _ in range(8)])
    idx4 = np.stack([np.random.permutation(U)[:I] for _ in range(8)])
    fd = mx_kscale(D)
    keysp = pack_weight(n((D, T)) / fd[:, None], "e4m3")
    notesp = pack_weight(n((D, U)) / fd[:, None], "e2m1")
    return {
        "query": (n((D, Q)) * 1.0 / np.sqrt(D) * fd[:, None]).astype(np.float32),
        "keys_words": keysp[0],
        "keys_scales": keysp[1],
        "notes_words": notesp[0],
        "notes_scales": notesp[1],
        "offs": striped8(idx),
        "offs2": striped8(idx2),
        "offs3": striped8(idx3),
        "offs4": striped8(idx4),
    }


def reference(query, keys_words, keys_scales, notes_words, notes_scales, offs, offs2, offs3, offs4):
    idx = unstriped8(offs)
    idx2 = unstriped8(offs2)
    idx3 = unstriped8(offs3)
    idx4 = unstriped8(offs4)
    keysu = unpack_weight(keys_words, keys_scales, "e4m3")
    notesu = unpack_weight(notes_words, notes_scales, "e2m1")
    queryq = mxq(f64(query), 0, "e4m3")
    a = queryq.T @ keysu
    b = queryq.T @ notesu
    w = np.minimum(pick8(a, idx, 16), pick8(b, idx2, 16))
    f1 = np.zeros((Q, T))
    f1[np.arange(Q)[:, None], idx[np.arange(Q) % 128 // 16]] = w
    f2 = np.zeros((Q, U))
    f2[np.arange(Q)[:, None], idx2[np.arange(Q) % 128 // 16]] = w
    a2 = a - f1
    b2 = b - f2
    y = np.maximum(pick8(a2, idx3, 16), pick8(b2, idx4, 16))
    return y

@@ -1,0 +1,117 @@
+from contextlib import ExitStack
+
+import concourse.mybir as mybir
+
+F32 = mybir.dt.float32
+BF16 = mybir.dt.bfloat16
+I32 = mybir.dt.int32
+U32 = mybir.dt.uint32
+U16 = mybir.dt.uint16
+U8 = mybir.dt.uint8
+FP8X4 = mybir.dt.float8_e4m3fn_x4
+FP4X4 = mybir.dt.float4_e2m1fn_x4
+ALU = mybir.AluOpType
+COPY = mybir.ActivationFunctionType.Copy
+
+P = 128
+D, T, U, I, Q = 512, 1024, 1024, 512, 128
+BANK = 512
+HALF = I // 2
+FLOPS = 2 * D * Q * (T + U)
+
+
+def tile_attend_toppled_two_kernel(tc, query, keys_words, keys_scales, notes_words, notes_scales,
+                                    offs, offs2, offs3, offs4, out):
+    nc = tc.nc
+    with ExitStack() as ctx:
+        sb = ctx.enter_context(tc.tile_pool(name="sb", bufs=1))
+        ps = ctx.enter_context(tc.psum_pool(name="ps", bufs=1))
+
+        q_raw = sb.tile([P, 4, Q], F32, name="q_raw")
+        nc.sync.dma_start(out=q_raw[:], in_=query.rearrange("(p j) q -> p j q", j=4))
+
+        n_scales = sb.tile([P, U], U8, name="n_scales", align_bytes=64)
+        k_scales = sb.tile([P, T], U8, name="k_scales", align_bytes=64)
+        for quad in range(4):
+            nc.scalar.dma_start(out=n_scales[32 * quad : 32 * quad + 4, :].bitcast(I32),
+                                in_=notes_scales[0, 4 * quad : 4 * quad + 4, :].bitcast(I32))
+
+        n_words = sb.tile([P, 2 * U], U8, name="n_words", align_bytes=64)
+        nc.sync.dma_start(out=n_words[:].bitcast(I32), in_=notes_words[0].bitcast(I32))
+        k_words = sb.tile([P, T], U32, name="k_words", align_bytes=64)
+        nc.sync.dma_start(out=k_words[:].bitcast(I32),
+                          in_=keys_words[0].rearrange("p n t -> p (n t)").bitcast(I32))
+        for quad in range(4):
+            nc.sync.dma_start(out=k_scales[32 * quad + 4 : 32 * quad + 8, :].bitcast(I32),
+                              in_=keys_scales[0, 4 * quad : 4 * quad + 4, :].bitcast(I32))
+
+        lists = []
+        for name, src in (("l2", offs2), ("l1", offs), ("l3", offs3), ("l4", offs4)):
+            tile = sb.tile([P, I // 16], U16, name=name)
+            nc.sync.dma_start(tile[:], src)
+            lists.append(tile)
+        l2, l1, l3, l4 = lists
+
+        f1 = sb.tile([P, T], F32, name="f1")
+        f2 = sb.tile([P, U], F32, name="f2")
+        nc.vector.memset(f1[:], 0.0)
+        nc.vector.memset(f2[:], 0.0)
+
+        q_bf = sb.tile([P, Q, 4], BF16, name="q_bf", align_bytes=64)
+        nc.vector.tensor_copy(out=q_bf[:].rearrange("p (c i) t -> p c t i", i=4),
+                              in_=q_raw[:].rearrange("p t (c i) -> p c t i", i=4))
+        q_words = sb.tile([P, Q], U32, name="q_words", align_bytes=64)
+        q_scales = sb.tile([P, Q], U8, name="q_scales", align_bytes=64)
+        nc.vector.quantize_mx(out=q_words[:].bitcast(FP8X4), scales=q_scales[:],
+                              in_=q_bf[:].rearrange("p q t -> p (q t)"))
+
+        def score(name, words, scales, width):
+            bank = ps.tile([P, width], F32, name=name)
+            nc.tensor.matmul_mx(out=bank[:], lhsT=q_words[:].bitcast(FP8X4), lhsT_scale=q_scales[:],
+                                rhs=words, rhs_scale=scales, start=True, stop=True)
+            return bank
+
+        a = sb.tile([P, T], F32, name="a")
+        b = sb.tile([P, U], F32, name="b")
+        b_spans = ((0, 512), (512, 768), (768, 1024))
+        b_banks = [score("b%d" % h, n_words[:, 2 * lo : 2 * hi].bitcast(FP4X4), n_scales[:, lo:hi], hi - lo)
+                   for h, (lo, hi) in enumerate(b_spans)]
+        a_banks = [score("a%d" % h, k_words[:, 256 * h : 256 * (h + 1)].bitcast(FP8X4),
+                         k_scales[4:P, 256 * h : 256 * (h + 1)], 256) for h in range(4)]
+        nc.scalar.copy(b[:, 0:512], b_banks[0][:])
+        nc.vector.tensor_copy(b[:, 512:768], b_banks[1][:])
+        nc.scalar.copy(b[:, 768:1024], b_banks[2][:])
+
+        gb = [sb.tile([P, HALF], F32, name="gb%d" % h) for h in range(2)]
+        cols = [slice(h * HALF // 16, (h + 1) * HALF // 16) for h in range(2)]
+        for h in range(4):
+            nc.vector.tensor_copy(a[:, 256 * h : 256 * (h + 1)], a_banks[h][:])
+        nc.scalar.activation(gb[0][:], b[:].indirect(l2[:, cols[0]]), COPY)
+        nc.scalar.activation(gb[1][:], b[:].indirect(l2[:, cols[1]]), COPY)
+
+        w = sb.tile([P, I], F32, name="w")
+        for h in range(2):
+            slots = slice(h * HALF, (h + 1) * HALF)
+            ga = sb.tile([P, HALF], F32, name="ga")
+            if h == 0:
+                nc.vector.tensor_copy(ga[:], a[:].indirect(l1[:, cols[h]]))
+            else:
+                nc.scalar.activation(ga[:], a[:].indirect(l1[:, cols[h]]), COPY)
+            nc.vector.tensor_tensor(w[:, slots], ga[:], gb[h][:], ALU.min)
+            nc.vector.tensor_copy(f1[:].indirect(l1[:, cols[h]]), w[:, slots])
+        a2 = sb.tile([P, T], F32, name="a2")
+        nc.gpsimd.tensor_tensor(a2[:], a[:], f1[:], ALU.subtract)
+        nc.vector.tensor_copy(f2[:].indirect(l2[:]), w[:])
+        g3 = sb.tile([P, I], F32, name="g3")
+        nc.scalar.activation(g3[:], a2[:].indirect(l3[:]), COPY)
+        b2 = sb.tile([P, U], F32, name="b2")
+        for bank, (lo, hi) in zip(b_banks, b_spans):
+            nc.vector.tensor_tensor(b2[:, lo:hi], bank[:], f2[:, lo:hi], ALU.subtract)
+        g4 = [sb.tile([P, HALF], F32, name="g4%d" % h) for h in range(2)]
+        nc.vector.tensor_copy(g4[0][:], b2[:].indirect(l4[:, cols[0]]))
+        nc.scalar.activation(g4[1][:], b2[:].indirect(l4[:, cols[1]]), COPY)
+        for h in range(2):
+            slots = slice(h * HALF, (h + 1) * HALF)
+            y = sb.tile([P, HALF], F32, name="y%d" % h)
+            nc.vector.tensor_tensor(y[:], g3[:, slots], g4[h][:], ALU.max)
+            (nc.sync, nc.scalar)[h].dma_start(out=out[:, slots], in_=y[:])

@@ -32,25 +32,26 @@ def tile_attend_toppled_two_kernel(tc, query, keys_words, keys_scales, notes_wor
 
         n_scales = sb.tile([P, U], U8, name="n_scales", align_bytes=64)
         k_scales = sb.tile([P, T], U8, name="k_scales", align_bytes=64)
-        for quad in range(4):
-            nc.scalar.dma_start(out=n_scales[32 * quad : 32 * quad + 4, :].bitcast(I32),
-                                in_=notes_scales[0, 4 * quad : 4 * quad + 4, :].bitcast(I32))
+        for r in range(4):
+            nc.sync.dma_start(out=n_scales[r:P:32, :].bitcast(I32), in_=notes_scales[0, r:16:4, :].bitcast(I32))
 
         n_words = sb.tile([P, 2 * U], U8, name="n_words", align_bytes=64)
         nc.sync.dma_start(out=n_words[:].bitcast(I32), in_=notes_words[0].bitcast(I32))
+        l2 = sb.tile([P, I // 16], U16, name="l2")
+        nc.sync.dma_start(l2[:], offs2)
         k_words = sb.tile([P, T], U32, name="k_words", align_bytes=64)
         nc.sync.dma_start(out=k_words[:].bitcast(I32),
                           in_=keys_words[0].rearrange("p n t -> p (n t)").bitcast(I32))
-        for quad in range(4):
-            nc.sync.dma_start(out=k_scales[32 * quad + 4 : 32 * quad + 8, :].bitcast(I32),
-                              in_=keys_scales[0, 4 * quad : 4 * quad + 4, :].bitcast(I32))
+        for r in range(4):
+            nc.sync.dma_start(out=k_scales[4 + r : P : 32, :].bitcast(I32),
+                              in_=keys_scales[0, r:16:4, :].bitcast(I32))
 
         lists = []
-        for name, src in (("l2", offs2), ("l1", offs), ("l3", offs3), ("l4", offs4)):
+        for name, src in (("l1", offs), ("l3", offs3), ("l4", offs4)):
             tile = sb.tile([P, I // 16], U16, name=name)
             nc.sync.dma_start(tile[:], src)
             lists.append(tile)
-        l2, l1, l3, l4 = lists
+        l1, l3, l4 = lists
 
         f1 = sb.tile([P, T], F32, name="f1")
         f2 = sb.tile([P, U], F32, name="f2")
@@ -58,12 +59,15 @@ def tile_attend_toppled_two_kernel(tc, query, keys_words, keys_scales, notes_wor
         nc.vector.memset(f2[:], 0.0)
 
         q_bf = sb.tile([P, Q, 4], BF16, name="q_bf", align_bytes=64)
-        nc.vector.tensor_copy(out=q_bf[:].rearrange("p (c i) t -> p c t i", i=4),
-                              in_=q_raw[:].rearrange("p t (c i) -> p c t i", i=4))
         q_words = sb.tile([P, Q], U32, name="q_words", align_bytes=64)
         q_scales = sb.tile([P, Q], U8, name="q_scales", align_bytes=64)
-        nc.vector.quantize_mx(out=q_words[:].bitcast(FP8X4), scales=q_scales[:],
-                              in_=q_bf[:].rearrange("p q t -> p (q t)"))
+        q_halves = (slice(0, Q // 2), slice(Q // 2, Q))
+        for rows in q_halves:
+            nc.vector.tensor_copy(out=q_bf[:, rows, :].rearrange("p (c i) t -> p c t i", i=4),
+                                  in_=q_raw[:, :, rows].rearrange("p t (c i) -> p c t i", i=4))
+        for rows in q_halves:
+            nc.vector.quantize_mx(out=q_words[:, rows].bitcast(FP8X4), scales=q_scales[:, rows],
+                                  in_=q_bf[:, rows, :].rearrange("p q t -> p (q t)"))
 
         def score(name, words, scales, width):
             bank = ps.tile([P, width], F32, name=name)
@@ -89,28 +93,26 @@ def tile_attend_toppled_two_kernel(tc, query, keys_words, keys_scales, notes_wor
         nc.scalar.activation(gb[0][:], b[:].indirect(l2[:, cols[0]]), COPY)
         nc.scalar.activation(gb[1][:], b[:].indirect(l2[:, cols[1]]), COPY)
 
+        ga = [sb.tile([P, HALF], F32, name="ga%d" % h) for h in range(2)]
+        nc.vector.tensor_copy(ga[0][:], a[:].indirect(l1[:, cols[0]]))
+        nc.scalar.activation(ga[1][:], a[:].indirect(l1[:, cols[1]]), COPY)
         w = sb.tile([P, I], F32, name="w")
-        for h in range(2):
-            slots = slice(h * HALF, (h + 1) * HALF)
-            ga = sb.tile([P, HALF], F32, name="ga")
-            if h == 0:
-                nc.vector.tensor_copy(ga[:], a[:].indirect(l1[:, cols[h]]))
-            else:
-                nc.scalar.activation(ga[:], a[:].indirect(l1[:, cols[h]]), COPY)
-            nc.vector.tensor_tensor(w[:, slots], ga[:], gb[h][:], ALU.min)
-            nc.vector.tensor_copy(f1[:].indirect(l1[:, cols[h]]), w[:, slots])
+        for h in (1, 0):
+            nc.vector.tensor_tensor(w[:, h * HALF : (h + 1) * HALF], ga[h][:], gb[h][:], ALU.min)
+        nc.vector.tensor_copy(f1[:].indirect(l1[:]), w[:])
         a2 = sb.tile([P, T], F32, name="a2")
         nc.gpsimd.tensor_tensor(a2[:], a[:], f1[:], ALU.subtract)
         nc.vector.tensor_copy(f2[:].indirect(l2[:]), w[:])
         g3 = sb.tile([P, I], F32, name="g3")
         nc.scalar.activation(g3[:], a2[:].indirect(l3[:]), COPY)
         b2 = sb.tile([P, U], F32, name="b2")
-        for bank, (lo, hi) in zip(b_banks, b_spans):
+        for bank, (lo, hi) in zip(b_banks[:2], b_spans[:2]):
             nc.vector.tensor_tensor(b2[:, lo:hi], bank[:], f2[:, lo:hi], ALU.subtract)
+        nc.gpsimd.tensor_tensor(b2[:, 768:U], b[:, 768:U], f2[:, 768:U], ALU.subtract)
         g4 = [sb.tile([P, HALF], F32, name="g4%d" % h) for h in range(2)]
         nc.vector.tensor_copy(g4[0][:], b2[:].indirect(l4[:, cols[0]]))
         nc.scalar.activation(g4[1][:], b2[:].indirect(l4[:, cols[1]]), COPY)
-        for h in range(2):
+        for h in (1, 0):
             slots = slice(h * HALF, (h + 1) * HALF)
             y = sb.tile([P, HALF], F32, name="y%d" % h)
             nc.vector.tensor_tensor(y[:], g3[:, slots], g4[h][:], ALU.max)

@@ -27,31 +27,31 @@ def tile_attend_toppled_two_kernel(tc, query, keys_words, keys_scales, notes_wor
         sb = ctx.enter_context(tc.tile_pool(name="sb", bufs=1))
         ps = ctx.enter_context(tc.psum_pool(name="ps", bufs=1))
 
-        q_raw = sb.tile([P, 4, Q], F32, name="q_raw")
-        nc.sync.dma_start(out=q_raw[:], in_=query.rearrange("(p j) q -> p j q", j=4))
-
         n_scales = sb.tile([P, U], U8, name="n_scales", align_bytes=64)
         k_scales = sb.tile([P, T], U8, name="k_scales", align_bytes=64)
-        for r in range(4):
-            nc.sync.dma_start(out=n_scales[r:P:32, :].bitcast(I32), in_=notes_scales[0, r:16:4, :].bitcast(I32))
 
+        def load_key_scales(queue, r):
+            queue.dma_start(out=k_scales[4 + r : P : 32, :].bitcast(I32), in_=keys_scales[0, r:16:4, :].bitcast(I32))
+
+        for r in range(4):
+            nc.scalar.dma_start(out=n_scales[r:P:32, :].bitcast(I32), in_=notes_scales[0, r:16:4, :].bitcast(I32))
+        q_raw = sb.tile([P, 4, Q], F32, name="q_raw")
+        nc.sync.dma_start(out=q_raw[:], in_=query.rearrange("(p j) q -> p j q", j=4))
         n_words = sb.tile([P, 2 * U], U8, name="n_words", align_bytes=64)
         nc.sync.dma_start(out=n_words[:].bitcast(I32), in_=notes_words[0].bitcast(I32))
-        l2 = sb.tile([P, I // 16], U16, name="l2")
-        nc.sync.dma_start(l2[:], offs2)
+        load_key_scales(nc.sync, 0)
         k_words = sb.tile([P, T], U32, name="k_words", align_bytes=64)
         nc.sync.dma_start(out=k_words[:].bitcast(I32),
                           in_=keys_words[0].rearrange("p n t -> p (n t)").bitcast(I32))
-        for r in range(4):
-            nc.sync.dma_start(out=k_scales[4 + r : P : 32, :].bitcast(I32),
-                              in_=keys_scales[0, r:16:4, :].bitcast(I32))
+        for r in range(1, 4):
+            load_key_scales(nc.scalar, r)
 
         lists = []
-        for name, src in (("l1", offs), ("l3", offs3), ("l4", offs4)):
+        for name, src in (("l2", offs2), ("l1", offs), ("l3", offs3), ("l4", offs4)):
             tile = sb.tile([P, I // 16], U16, name=name)
             nc.sync.dma_start(tile[:], src)
             lists.append(tile)
-        l1, l3, l4 = lists
+        l2, l1, l3, l4 = lists
 
         f1 = sb.tile([P, T], F32, name="f1")
         f2 = sb.tile([P, U], F32, name="f2")

@@ -27,24 +27,21 @@ def tile_attend_toppled_two_kernel(tc, query, keys_words, keys_scales, notes_wor
         sb = ctx.enter_context(tc.tile_pool(name="sb", bufs=1))
         ps = ctx.enter_context(tc.psum_pool(name="ps", bufs=1))
 
-        n_scales = sb.tile([P, U], U8, name="n_scales", align_bytes=64)
-        k_scales = sb.tile([P, T], U8, name="k_scales", align_bytes=64)
-
-        def load_key_scales(queue, r):
-            queue.dma_start(out=k_scales[4 + r : P : 32, :].bitcast(I32), in_=keys_scales[0, r:16:4, :].bitcast(I32))
-
-        for r in range(4):
-            nc.scalar.dma_start(out=n_scales[r:P:32, :].bitcast(I32), in_=notes_scales[0, r:16:4, :].bitcast(I32))
         q_raw = sb.tile([P, 4, Q], F32, name="q_raw")
         nc.sync.dma_start(out=q_raw[:], in_=query.rearrange("(p j) q -> p j q", j=4))
+
+        n_scales = sb.tile([P, U], U8, name="n_scales", align_bytes=64)
+        k_scales = sb.tile([P, T], U8, name="k_scales", align_bytes=64)
+        for r in range(4):
+            nc.sync.dma_start(out=n_scales[r:P:32, :].bitcast(I32), in_=notes_scales[0, r:16:4, :].bitcast(I32))
+
         n_words = sb.tile([P, 2 * U], U8, name="n_words", align_bytes=64)
         nc.sync.dma_start(out=n_words[:].bitcast(I32), in_=notes_words[0].bitcast(I32))
-        load_key_scales(nc.sync, 0)
         k_words = sb.tile([P, T], U32, name="k_words", align_bytes=64)
         nc.sync.dma_start(out=k_words[:].bitcast(I32),
                           in_=keys_words[0].rearrange("p n t -> p (n t)").bitcast(I32))
-        for r in range(1, 4):
-            load_key_scales(nc.scalar, r)
+        for r, queue in enumerate((nc.sync, nc.sync, nc.sync, nc.gpsimd)):
+            queue.dma_start(out=k_scales[4 + r : P : 32, :].bitcast(I32), in_=keys_scales[0, r:16:4, :].bitcast(I32))
 
         lists = []
         for name, src in (("l2", offs2), ("l1", offs), ("l3", offs3), ("l4", offs4)):
@@ -53,21 +50,21 @@ def tile_attend_toppled_two_kernel(tc, query, keys_words, keys_scales, notes_wor
             lists.append(tile)
         l2, l1, l3, l4 = lists
 
-        f1 = sb.tile([P, T], F32, name="f1")
-        f2 = sb.tile([P, U], F32, name="f2")
-        nc.vector.memset(f1[:], 0.0)
-        nc.vector.memset(f2[:], 0.0)
-
-        q_bf = sb.tile([P, Q, 4], BF16, name="q_bf", align_bytes=64)
         q_words = sb.tile([P, Q], U32, name="q_words", align_bytes=64)
         q_scales = sb.tile([P, Q], U8, name="q_scales", align_bytes=64)
         q_halves = (slice(0, Q // 2), slice(Q // 2, Q))
-        for rows in q_halves:
-            nc.vector.tensor_copy(out=q_bf[:, rows, :].rearrange("p (c i) t -> p c t i", i=4),
+        q_bf = [sb.tile([P, Q // 2, 4], BF16, name="q_bf%d" % h, tag="shared%d" % h, align_bytes=64) for h in range(2)]
+        for h, rows in enumerate(q_halves):
+            nc.vector.tensor_copy(out=q_bf[h][:].rearrange("p (c i) t -> p c t i", i=4),
                                   in_=q_raw[:, :, rows].rearrange("p t (c i) -> p c t i", i=4))
-        for rows in q_halves:
+        for h, rows in enumerate(q_halves):
             nc.vector.quantize_mx(out=q_words[:, rows].bitcast(FP8X4), scales=q_scales[:, rows],
-                                  in_=q_bf[:, rows, :].rearrange("p q t -> p (q t)"))
+                                  in_=q_bf[h][:].rearrange("p q t -> p (q t)"))
+
+        f1 = sb.tile([P, T], F32, name="f1", tag="shared0", align_bytes=64)
+        f2 = sb.tile([P, U], F32, name="f2", tag="shared1", align_bytes=64)
+        nc.vector.memset(f1[:], 0.0)
+        nc.vector.memset(f2[:], 0.0)
 
         def score(name, words, scales, width):
             bank = ps.tile([P, width], F32, name=name)

from contextlib import ExitStack

import concourse.mybir as mybir

F32 = mybir.dt.float32
BF16 = mybir.dt.bfloat16
I32 = mybir.dt.int32
U32 = mybir.dt.uint32
U16 = mybir.dt.uint16
U8 = mybir.dt.uint8
FP8X4 = mybir.dt.float8_e4m3fn_x4
FP4X4 = mybir.dt.float4_e2m1fn_x4
ALU = mybir.AluOpType
COPY = mybir.ActivationFunctionType.Copy

P = 128
D, T, U, I, Q = 512, 1024, 1024, 512, 128
BANK = 512
HALF = I // 2
FLOPS = 2 * D * Q * (T + U)


def tile_attend_toppled_two_kernel(tc, query, keys_words, keys_scales, notes_words, notes_scales,
                                    offs, offs2, offs3, offs4, out):
    nc = tc.nc
    with ExitStack() as ctx:
        sb = ctx.enter_context(tc.tile_pool(name="sb", bufs=1))
        ps = ctx.enter_context(tc.psum_pool(name="ps", bufs=1))

        q_raw = sb.tile([P, 4, Q], F32, name="q_raw")
        nc.sync.dma_start(out=q_raw[:], in_=query.rearrange("(p j) q -> p j q", j=4))

        n_scales = sb.tile([P, U], U8, name="n_scales", align_bytes=64)
        k_scales = sb.tile([P, T], U8, name="k_scales", align_bytes=64)
        for r in range(4):
            nc.sync.dma_start(out=n_scales[r:P:32, :].bitcast(I32), in_=notes_scales[0, r:16:4, :].bitcast(I32))

        n_words = sb.tile([P, 2 * U], U8, name="n_words", align_bytes=64)
        nc.sync.dma_start(out=n_words[:].bitcast(I32), in_=notes_words[0].bitcast(I32))
        k_words = sb.tile([P, T], U32, name="k_words", align_bytes=64)
        nc.sync.dma_start(out=k_words[:].bitcast(I32),
                          in_=keys_words[0].rearrange("p n t -> p (n t)").bitcast(I32))
        for r, queue in enumerate((nc.sync, nc.sync, nc.sync, nc.gpsimd)):
            queue.dma_start(out=k_scales[4 + r : P : 32, :].bitcast(I32), in_=keys_scales[0, r:16:4, :].bitcast(I32))

        lists = []
        for name, src in (("l2", offs2), ("l1", offs), ("l3", offs3), ("l4", offs4)):
            tile = sb.tile([P, I // 16], U16, name=name)
            nc.sync.dma_start(tile[:], src)
            lists.append(tile)
        l2, l1, l3, l4 = lists

        q_words = sb.tile([P, Q], U32, name="q_words", align_bytes=64)
        q_scales = sb.tile([P, Q], U8, name="q_scales", align_bytes=64)
        q_halves = (slice(0, Q // 2), slice(Q // 2, Q))
        q_bf = [sb.tile([P, Q // 2, 4], BF16, name="q_bf%d" % h, tag="shared%d" % h, align_bytes=64) for h in range(2)]
        for h, rows in enumerate(q_halves):
            nc.vector.tensor_copy(out=q_bf[h][:].rearrange("p (c i) t -> p c t i", i=4),
                                  in_=q_raw[:, :, rows].rearrange("p t (c i) -> p c t i", i=4))
        for h, rows in enumerate(q_halves):
            nc.vector.quantize_mx(out=q_words[:, rows].bitcast(FP8X4), scales=q_scales[:, rows],
                                  in_=q_bf[h][:].rearrange("p q t -> p (q t)"))

        f1 = sb.tile([P, T], F32, name="f1", tag="shared0", align_bytes=64)
        f2 = sb.tile([P, U], F32, name="f2", tag="shared1", align_bytes=64)
        nc.vector.memset(f1[:], 0.0)
        nc.vector.memset(f2[:], 0.0)

        def score(name, words, scales, width):
            bank = ps.tile([P, width], F32, name=name)
            nc.tensor.matmul_mx(out=bank[:], lhsT=q_words[:].bitcast(FP8X4), lhsT_scale=q_scales[:],
                                rhs=words, rhs_scale=scales, start=True, stop=True)
            return bank

        a = sb.tile([P, T], F32, name="a")
        b = sb.tile([P, U], F32, name="b")
        b_spans = ((0, 512), (512, 768), (768, 1024))
        b_banks = [score("b%d" % h, n_words[:, 2 * lo : 2 * hi].bitcast(FP4X4), n_scales[:, lo:hi], hi - lo)
                   for h, (lo, hi) in enumerate(b_spans)]
        a_banks = [score("a%d" % h, k_words[:, 256 * h : 256 * (h + 1)].bitcast(FP8X4),
                         k_scales[4:P, 256 * h : 256 * (h + 1)], 256) for h in range(4)]
        nc.scalar.copy(b[:, 0:512], b_banks[0][:])
        nc.vector.tensor_copy(b[:, 512:768], b_banks[1][:])
        nc.scalar.copy(b[:, 768:1024], b_banks[2][:])

        gb = [sb.tile([P, HALF], F32, name="gb%d" % h) for h in range(2)]
        cols = [slice(h * HALF // 16, (h + 1) * HALF // 16) for h in range(2)]
        for h in range(4):
            nc.vector.tensor_copy(a[:, 256 * h : 256 * (h + 1)], a_banks[h][:])
        nc.scalar.activation(gb[0][:], b[:].indirect(l2[:, cols[0]]), COPY)
        nc.scalar.activation(gb[1][:], b[:].indirect(l2[:, cols[1]]), COPY)

        ga = [sb.tile([P, HALF], F32, name="ga%d" % h) for h in range(2)]
        nc.vector.tensor_copy(ga[0][:], a[:].indirect(l1[:, cols[0]]))
        nc.scalar.activation(ga[1][:], a[:].indirect(l1[:, cols[1]]), COPY)
        w = sb.tile([P, I], F32, name="w")
        for h in (1, 0):
            nc.vector.tensor_tensor(w[:, h * HALF : (h + 1) * HALF], ga[h][:], gb[h][:], ALU.min)
        nc.vector.tensor_copy(f1[:].indirect(l1[:]), w[:])
        a2 = sb.tile([P, T], F32, name="a2")
        nc.gpsimd.tensor_tensor(a2[:], a[:], f1[:], ALU.subtract)
        nc.vector.tensor_copy(f2[:].indirect(l2[:]), w[:])
        g3 = sb.tile([P, I], F32, name="g3")
        nc.scalar.activation(g3[:], a2[:].indirect(l3[:]), COPY)
        b2 = sb.tile([P, U], F32, name="b2")
        for bank, (lo, hi) in zip(b_banks[:2], b_spans[:2]):
            nc.vector.tensor_tensor(b2[:, lo:hi], bank[:], f2[:, lo:hi], ALU.subtract)
        nc.gpsimd.tensor_tensor(b2[:, 768:U], b[:, 768:U], f2[:, 768:U], ALU.subtract)
        g4 = [sb.tile([P, HALF], F32, name="g4%d" % h) for h in range(2)]
        nc.vector.tensor_copy(g4[0][:], b2[:].indirect(l4[:, cols[0]]))
        nc.scalar.activation(g4[1][:], b2[:].indirect(l4[:, cols[1]]), COPY)
        for h in (1, 0):
            slots = slice(h * HALF, (h + 1) * HALF)
            y = sb.tile([P, HALF], F32, name="y%d" % h)
            nc.vector.tensor_tensor(y[:], g3[:, slots], g4[h][:], ALU.max)
            (nc.sync, nc.scalar)[h].dma_start(out=out[:, slots], in_=y[:])
